import numpy as np
import ml_dtypes


def mxq(x, axis, fmt="e4m3"):
    dtype, down = {"e4m3": (ml_dtypes.float8_e4m3fn, 7), "e5m2": (ml_dtypes.float8_e5m2, 14)}[fmt]
    v = np.moveaxis(np.asarray(x, np.float32).astype(ml_dtypes.bfloat16).astype(np.float64), axis, -1)
    blocks = v.reshape(v.shape[:-1] + (-1, 32))
    amax = np.abs(blocks).max(-1, keepdims=True)
    byte = np.maximum(np.where(amax > 0, np.frexp(amax)[1] - 1 + 127, 0) - down, 1)
    scale = np.exp2(byte - 127.0)
    codes = (blocks / scale).astype(np.float32).astype(dtype).astype(np.float64)
    return np.moveaxis((codes * scale).reshape(v.shape), -1, axis)


WIDE = False


def mx_kscale(k):
    if not WIDE:
        return np.ones(k)
    levels = np.array([10, -10, 5, -5, 0])
    if k % 512:
        return np.exp2(np.random.permutation(np.resize(levels, k // 32))).repeat(32)
    a = np.empty((k // 512, 16))
    for p in range(k // 512):
        a[p, :8] = np.random.permutation(np.resize(levels, 8))
        for g in range(8):
            far = levels[np.abs(levels - a[p, g]) >= 10]
            a[p, g + 8] = far[np.random.randint(len(far))]
    return np.exp2(a.ravel()).repeat(32)


def f64(x):
    return np.asarray(x).astype(np.float64)


def striped(idx):
    return np.tile(idx.reshape(-1, 16).T, (8, 1)).astype(np.uint16)


def unstriped(offs):
    return offs[:16].T.reshape(-1).astype(np.int64)


def striped8(idx):
    return np.concatenate([x.reshape(-1, 16).T for x in idx]).astype(np.uint16)


def runs(offs, k):
    lists = np.stack([offs[16 * r : 16 * r + 16].T.reshape(-1) for r in range(8)]).astype(np.int64)
    return lists[np.arange(k) % 512 // 64]


def pack_weight(w):
    k, n = w.shape
    w = f64(np.asarray(w, np.float32).astype(ml_dtypes.bfloat16)).reshape(k // 32, 32, n)
    amax = np.abs(w).max(1)
    byte = np.clip(np.where(amax > 0, np.frexp(amax)[1] - 1 + 127 - 7, 1), 1, 254)
    scaled = (w * np.exp2(127.0 - byte)[:, None, :]).reshape(k, n).astype(np.float32)
    words = np.ascontiguousarray(scaled.reshape(k // 512, 128, 4, n).transpose(0, 1, 3, 2)).astype(ml_dtypes.float8_e4m3fn).view(np.uint8)
    return words, np.ascontiguousarray(byte.astype(np.uint8).reshape(k // 512, 16, n))


def unpack_weight(words, scales):
    g, p, n, _ = words.shape
    vals = np.ascontiguousarray(words).view(ml_dtypes.float8_e4m3fn).astype(np.float64) * np.repeat(np.exp2(scales.astype(np.float64) - 127.0), 8, axis=1)[..., None]
    return vals.transpose(0, 1, 3, 2).reshape(g * 512, n)


def sigmoid(v):
    return 1.0 / (1.0 + np.exp(-np.maximum(v, -700.0)))


K, T, S, N, H, W = 512, 2048, 512, 512, 512, 2048


def setup_inputs():
    n = np.random.standard_normal
    s = mx_kscale(K)[:, None]
    u = mx_kscale(H)
    packed_xT = pack_weight(n((K, T)) * s)
    return {
        "x_words": packed_xT[0],
        "x_scales": packed_xT[1],
        "w1": (n((K, H)) / np.sqrt(K) / s).astype(np.float32),
        "tau": np.random.uniform(0.5, 1.2, (H, 1)).astype(np.float32),
        "gn": (np.random.uniform(0.5, 1.5, (H, 1)) * u[:, None]).astype(np.float32),
        "w2": (n((H, N)) / np.sqrt(H) / u[:, None]).astype(np.float32),
        "sl": np.random.uniform(1.5, 3.0, (N, 1)).astype(np.float32),
        "th": (0.5 * n((N, 1))).astype(np.float32),
        "offs": striped(np.random.permutation(T)[:S]),
        "n1": striped8(np.stack([np.random.permutation(S) for _ in range(8)])),
        "n2": striped8(np.stack([np.random.permutation(S) for _ in range(8)])),
        "n3": striped(np.random.randint(0, S, W)),
    }


def reference(x_words, x_scales, w1, tau, gn, w2, sl, th, offs, n1, n2, n3):
    xq = unpack_weight(x_words, x_scales)[:, unstriped(offs)]
    y = mxq(f64(w1), 0, "e4m3").T @ xq
    sz = np.abs(y)
    ea = np.exp(-1.0 * (f64(tau) * (sz[np.arange(H)[:, None], runs(n1, H)])))
    z = f64(gn) * ((y - (y[np.arange(H)[:, None], runs(n2, H)])) * ea)
    h = mxq(f64(w2), 0, "e4m3").T @ mxq(z, 0, "e4m3")
    sg = sigmoid(f64(sl) * (h[:, unstriped(n3)] - f64(th)))
    cnt = sg.reshape(N, S, 4).sum(axis=2)
    return np.maximum(h, cnt + -1.5)

@@ -1,0 +1,224 @@
+from contextlib import ExitStack
+
+import concourse.mybir as mybir
+
+K, T, S, N, H, W = 512, 2048, 512, 512, 512, 2048
+FLOPS = 2 * K * H * S + 2 * H * N * S
+
+F32 = mybir.dt.float32
+BF16 = mybir.dt.bfloat16
+I32 = mybir.dt.int32
+U32 = mybir.dt.uint32
+U16 = mybir.dt.uint16
+U8 = mybir.dt.uint8
+FP8X4 = mybir.dt.float8_e4m3fn_x4
+ALU = mybir.AluOpType
+ACT = mybir.ActivationFunctionType
+
+P = 128
+PACK = 4
+GROUP = 16
+HALF = S // 2
+Z_CHUNKS = ((0, 256), (256, 384), (384, 512))
+W1_VECTOR_ROWS = 80
+
+
+def entries(lst, lo, hi):
+    return lst[:, lo // GROUP : hi // GROUP]
+
+
+def tile_picked_layelaegc_none_p_kernel(
+    tc, x_words, x_scales, w1, tau, gn, w2, sl, th, offs, n1, n2, n3, out
+):
+    nc = tc.nc
+    with ExitStack() as ctx:
+        held = ctx.enter_context(tc.tile_pool(name="held", bufs=1))
+        ring = ctx.enter_context(tc.tile_pool(name="ring", bufs=8))
+        psum = ctx.enter_context(tc.psum_pool(name="psum", bufs=1))
+
+        offs_t = held.tile([P, S // GROUP], U16, name="offs_t")
+        n1_t = held.tile([P, S // GROUP], U16, name="n1_t")
+        n2_t = held.tile([P, S // GROUP], U16, name="n2_t")
+        n3_t = held.tile([P, W // GROUP], U16, name="n3_t")
+
+        xw = held.tile([P, T], U32, name="xw", align_bytes=64)
+        xs = held.tile([P, T], U8, name="xs", align_bytes=64)
+        w1_raw = held.tile([P, PACK, H], F32, name="w1_raw", align_bytes=64)
+        w2_first = held.tile([P, PACK, P], F32, name="w2_first", align_bytes=64)
+        w2_rest = held.tile([P, PACK, N - P], F32, name="w2_rest", align_bytes=64)
+        tau_t = held.tile([P, PACK], F32, name="tau_t")
+        gn_t = held.tile([P, PACK], F32, name="gn_t")
+        sl_t = held.tile([P, PACK], F32, name="sl_t")
+        th_t = held.tile([P, PACK], F32, name="th_t")
+
+        nc.vector.memset(xs[:].bitcast(I32), 0)
+        w2_rows = w2.rearrange("(p j) n -> p j n", j=PACK)
+        nc.sync.dma_start(out=w1_raw[:], in_=w1.rearrange("(p j) n -> p j n", j=PACK))
+        nc.sync.dma_start(offs_t[:], offs)
+        for q in range(4):
+            nc.sync.dma_start(
+                out=xs[32 * q : 32 * q + 4, :].bitcast(I32),
+                in_=x_scales[0, 4 * q : 4 * q + 4, :].bitcast(I32),
+            )
+        nc.sync.dma_start(
+            out=xw[:].bitcast(I32),
+            in_=x_words[0].rearrange("p n t -> p (n t)").bitcast(I32),
+        )
+        nc.sync.dma_start(out=gn_t[:], in_=gn.rearrange("(p t) o -> p (t o)", t=PACK))
+        nc.sync.dma_start(out=w2_first[:], in_=w2_rows[:, :, 0:P])
+        nc.sync.dma_start(n2_t[:], n2)
+        nc.sync.dma_start(out=tau_t[:], in_=tau.rearrange("(p t) o -> p (t o)", t=PACK))
+        nc.sync.dma_start(n1_t[:], n1)
+        nc.sync.dma_start(out=w2_rest[:], in_=w2_rows[:, :, P:N])
+        nc.sync.dma_start(n3_t[:], n3)
+        with nc.allow_non_contiguous_dma(reason="one value a row"):
+            nc.sync.dma_start(out=sl_t[:], in_=sl.rearrange("(t p) o -> p (t o)", p=P))
+            nc.sync.dma_start(out=th_t[:], in_=th.rearrange("(t p) o -> p (t o)", p=P))
+
+        w1_bf = held.tile([P, PACK * H], BF16, name="w1_bf", tag="w1_bf_then_xw_g", align_bytes=64)
+        w1_dst = w1_bf[:].rearrange("p (t m j) -> p m j t", t=PACK, j=PACK)
+        w1_src = w1_raw[:].rearrange("p j (m t) -> p m j t", t=PACK)
+        nc.vector.tensor_copy(out=w1_dst[:, 0:W1_VECTOR_ROWS], in_=w1_src[:, 0:W1_VECTOR_ROWS])
+        nc.scalar.activation(out=w1_dst[:, W1_VECTOR_ROWS:P], in_=w1_src[:, W1_VECTOR_ROWS:P], func=ACT.Copy)
+        xs_g = held.tile([P, S], U8, name="xs_g", align_bytes=64)
+        nc.vector.tensor_copy(xs_g[:], xs[:].indirect(offs_t[:]))
+
+        w1_q = held.tile([P, H], U32, name="w1_q", align_bytes=64)
+        w1_s = held.tile([P, H], U8, name="w1_s", align_bytes=64)
+        nc.vector.quantize_mx(out=w1_q[:].bitcast(FP8X4), scales=w1_s[:], in_=w1_bf[:])
+
+        xw_g = held.tile([P, S], U32, name="xw_g", tag="w1_bf_then_xw_g", align_bytes=64)
+        for lo in (0, HALF):
+            nc.vector.tensor_copy(xw_g[:, lo : lo + HALF], xw[:].indirect(entries(offs_t, lo, lo + HALF)))
+        y_banks = [psum.tile([P, S], F32, name=f"y_bank{t}") for t in range(PACK)]
+        for t in range(PACK):
+            rows = slice(t * P, (t + 1) * P)
+            for cols in ([slice(0, HALF), slice(HALF, S)] if t == 0 else [slice(0, S)]):
+                nc.tensor.matmul_mx(
+                    out=y_banks[t][:, cols],
+                    lhsT=w1_q[:, rows].bitcast(FP8X4),
+                    lhsT_scale=w1_s[:, rows],
+                    rhs=xw_g[:, cols].bitcast(FP8X4),
+                    rhs_scale=xs_g[:, cols],
+                    start=True,
+                    stop=True,
+                )
+
+        w2_q = held.tile([P, N], U32, name="w2_q", align_bytes=64)
+        w2_s = held.tile([P, N], U8, name="w2_s", align_bytes=64)
+
+        def quantize_w2(t, src, staged):
+            nc.vector.tensor_copy(
+                out=staged[:].rearrange("p (c i j) -> p c j i", i=4, j=PACK),
+                in_=src.rearrange("p j (c i) -> p c j i", i=4),
+            )
+            nc.vector.quantize_mx(
+                out=w2_q[:, t * P : (t + 1) * P].bitcast(FP8X4),
+                scales=w2_s[:, t * P : (t + 1) * P],
+                in_=staged[:],
+            )
+
+        w2_bf0 = held.tile([P, PACK * P], BF16, name="w2_bf0", align_bytes=64)
+        quantize_w2(0, w2_first[:], w2_bf0)
+
+        neg_tau = held.tile([P, PACK], F32, name="neg_tau")
+        nc.vector.tensor_scalar(neg_tau[:], tau_t[:], -1.0, None, ALU.mult)
+
+        gy = [held.tile([P, S], F32, name=f"gy{t}", align_bytes=64) for t in range(PACK)]
+        sz = [held.tile([P, S], F32, name=f"sz{t}", align_bytes=64) for t in range(PACK)]
+        h_win = [held.tile([P, 2 * S], F32, name=f"h_win{t}", align_bytes=64) for t in range(PACK)]
+        diff = held.tile([P, PACK, S], F32, name="diff", align_bytes=64)
+        ea = held.tile([P, PACK, S], F32, name="ea", align_bytes=64)
+
+        for t in range(PACK + 1):
+            if t < PACK:
+                nc.scalar.activation(out=gy[t][:], in_=y_banks[t][:], func=ACT.Copy, scale=gn_t[:, t : t + 1])
+            if t > 0:
+                nc.scalar.activation(out=sz[t - 1][:], in_=y_banks[t - 1][:], func=ACT.Abs)
+        for t in range(PACK):
+            for lo in (0, HALF):
+                looked_up = gy[t][:].indirect(entries(n2_t, lo, lo + HALF))
+                if t == PACK - 1 and lo == HALF:
+                    nc.scalar.activation(out=h_win[t][:, S + lo : S + lo + HALF], in_=looked_up, func=ACT.Copy)
+                else:
+                    nc.vector.tensor_copy(h_win[t][:, S + lo : S + lo + HALF], looked_up)
+            for lo in (0, HALF):
+                nc.vector.tensor_tensor(
+                    diff[:, t, lo : lo + HALF],
+                    gy[t][:, lo : lo + HALF],
+                    h_win[t][:, S + lo : S + lo + HALF],
+                    ALU.subtract,
+                )
+
+        z_q = held.tile([P, S], U32, name="z_q", align_bytes=64)
+        z_s = held.tile([P, S], U8, name="z_s", align_bytes=64)
+        h_banks = [psum.tile([P, S], F32, name=f"h_bank{t}") for t in range(PACK)]
+
+        def second_product(t, lo, hi):
+            rows = slice(t * P, (t + 1) * P)
+            nc.tensor.matmul_mx(
+                out=h_banks[t][:, lo:hi],
+                lhsT=w2_q[:, rows].bitcast(FP8X4),
+                lhsT_scale=w2_s[:, rows],
+                rhs=z_q[:, lo:hi].bitcast(FP8X4),
+                rhs_scale=z_s[:, lo:hi],
+                start=True,
+                stop=True,
+            )
+            nc.vector.tensor_copy(out=h_win[t][:, lo:hi], in_=h_banks[t][:, lo:hi])
+
+        for c, (lo, hi) in enumerate(Z_CHUNKS):
+            for t in range(PACK):
+                nc.scalar.activation(
+                    out=ea[:, t, lo:hi],
+                    in_=sz[t][:].indirect(entries(n1_t, lo, hi)),
+                    func=ACT.Exp,
+                    scale=neg_tau[:, t : t + 1],
+                )
+            parts = [(a, a + P) for a in range(lo, hi, P)]
+            z_bf = [held.tile([P, PACK * P], BF16, name=f"z_bf{a}", tag=f"z_bf{a}", align_bytes=64) for a, b in parts]
+            for (a, b), zb in zip(parts, z_bf):
+                nc.vector.tensor_tensor(
+                    zb[:].rearrange("p (c i t) -> p c t i", i=2, t=PACK),
+                    diff[:, :, a:b].rearrange("p t (c i) -> p c t i", i=2),
+                    ea[:, :, a:b].rearrange("p t (c i) -> p c t i", i=2),
+                    ALU.mult,
+                )
+            for (a, b), zb in zip(parts, z_bf):
+                nc.vector.quantize_mx(out=z_q[:, a:b].bitcast(FP8X4), scales=z_s[:, a:b], in_=zb[:])
+            second_product(0, lo, hi)
+
+        bias = held.tile([P, PACK], F32, name="bias")
+        nc.vector.scalar_tensor_tensor(bias[:], sl_t[:], -1.0, th_t[:], ALU.mult, ALU.mult)
+
+        def next_rows(t):
+            staged = held.tile([P, PACK * P], BF16, name=f"w2_bf{t}", tag="z_bf384", align_bytes=64)
+            quantize_w2(t, w2_rest[:, :, (t - 1) * P : t * P], staged)
+            second_product(t, 0, S)
+
+        for t in range(1, PACK):
+            next_rows(t)
+
+        for t in range(PACK):
+            res = held.tile([P, S], F32, name=f"res{t}")
+            cuts = [0, 128, 256, 384, 512] if t < PACK - 1 else [0, 128, 256, 384, 448, 512]
+            stored = 0
+            for lo, hi in zip(cuts[:-1], cuts[1:]):
+                sg = ring.tile([P, 4 * (hi - lo)], F32, name="sg")
+                nc.scalar.activation(
+                    out=sg[:],
+                    in_=h_win[t][:].indirect(entries(n3_t, 4 * lo, 4 * hi)),
+                    func=ACT.Sigmoid,
+                    scale=sl_t[:, t : t + 1],
+                    bias=bias[:, t : t + 1],
+                )
+                cnt = ring.tile([P, hi - lo], F32, name="cnt")
+                nc.vector.tensor_reduce(
+                    cnt[:], sg[:].rearrange("p (j d) -> p j d", d=4), mybir.AxisListType.X, ALU.add
+                )
+                nc.vector.scalar_tensor_tensor(
+                    res[:, lo:hi], cnt[:], -1.5, h_win[t][:, lo:hi], ALU.add, ALU.max
+                )
+                if hi == S or (t == PACK - 1 and hi >= 384):
+                    nc.sync.dma_start(out=out[t * P : (t + 1) * P, stored:hi], in_=res[:, stored:hi])
+                    stored = hi

@@ -33,7 +33,7 @@ def tile_picked_layelaegc_none_p_kernel(
     nc = tc.nc
     with ExitStack() as ctx:
         held = ctx.enter_context(tc.tile_pool(name="held", bufs=1))
-        ring = ctx.enter_context(tc.tile_pool(name="ring", bufs=8))
+        ring = ctx.enter_context(tc.tile_pool(name="ring", bufs=5))
         psum = ctx.enter_context(tc.psum_pool(name="psum", bufs=1))
 
         offs_t = held.tile([P, S // GROUP], U16, name="offs_t")
@@ -52,9 +52,14 @@ def tile_picked_layelaegc_none_p_kernel(
         th_t = held.tile([P, PACK], F32, name="th_t")
 
         nc.vector.memset(xs[:].bitcast(I32), 0)
+        h_win = [
+            held.tile([P, (4 if t < PACK - 1 else 2) * S], F32, name=f"h_win{t}", align_bytes=64) for t in range(PACK)
+        ]
+        for t in range(PACK - 1):
+            nc.vector.memset(h_win[t][:, 2 * S : 4 * S], 0.0)
         w2_rows = w2.rearrange("(p j) n -> p j n", j=PACK)
-        nc.sync.dma_start(out=w1_raw[:], in_=w1.rearrange("(p j) n -> p j n", j=PACK))
         nc.sync.dma_start(offs_t[:], offs)
+        nc.sync.dma_start(out=w1_raw[:], in_=w1.rearrange("(p j) n -> p j n", j=PACK))
         for q in range(4):
             nc.sync.dma_start(
                 out=xs[32 * q : 32 * q + 4, :].bitcast(I32),
@@ -90,19 +95,20 @@ def tile_picked_layelaegc_none_p_kernel(
         xw_g = held.tile([P, S], U32, name="xw_g", tag="w1_bf_then_xw_g", align_bytes=64)
         for lo in (0, HALF):
             nc.vector.tensor_copy(xw_g[:, lo : lo + HALF], xw[:].indirect(entries(offs_t, lo, lo + HALF)))
-        y_banks = [psum.tile([P, S], F32, name=f"y_bank{t}") for t in range(PACK)]
-        for t in range(PACK):
+        y_bank = {(0, 0): psum.tile([P, HALF], F32, name="y0_low", tag="bank0"), (0, HALF): psum.tile([P, HALF], F32, name="y0_high", tag="bank1")}
+        for t in range(1, PACK):
+            y_bank[t, 0] = psum.tile([P, S], F32, name=f"y{t}", tag=f"bank{t + 1}")
+        for t, lo, hi in [(0, 0, HALF), (1, 0, HALF), (0, HALF, S), (1, HALF, S), (2, 0, S), (3, 0, S)]:
             rows = slice(t * P, (t + 1) * P)
-            for cols in ([slice(0, HALF), slice(HALF, S)] if t == 0 else [slice(0, S)]):
-                nc.tensor.matmul_mx(
-                    out=y_banks[t][:, cols],
-                    lhsT=w1_q[:, rows].bitcast(FP8X4),
-                    lhsT_scale=w1_s[:, rows],
-                    rhs=xw_g[:, cols].bitcast(FP8X4),
-                    rhs_scale=xs_g[:, cols],
-                    start=True,
-                    stop=True,
-                )
+            nc.tensor.matmul_mx(
+                out=y_bank[t, lo][:] if t == 0 else y_bank[t, 0][:, lo:hi],
+                lhsT=w1_q[:, rows].bitcast(FP8X4),
+                lhsT_scale=w1_s[:, rows],
+                rhs=xw_g[:, lo:hi].bitcast(FP8X4),
+                rhs_scale=xs_g[:, lo:hi],
+                start=True,
+                stop=True,
+            )
 
         w2_q = held.tile([P, N], U32, name="w2_q", align_bytes=64)
         w2_s = held.tile([P, N], U8, name="w2_s", align_bytes=64)
@@ -126,23 +132,38 @@ def tile_picked_layelaegc_none_p_kernel(
 
         gy = [held.tile([P, S], F32, name=f"gy{t}", align_bytes=64) for t in range(PACK)]
         sz = [held.tile([P, S], F32, name=f"sz{t}", align_bytes=64) for t in range(PACK)]
-        h_win = [held.tile([P, 2 * S], F32, name=f"h_win{t}", align_bytes=64) for t in range(PACK)]
         diff = held.tile([P, PACK, S], F32, name="diff", align_bytes=64)
         ea = held.tile([P, PACK, S], F32, name="ea", align_bytes=64)
 
-        for t in range(PACK + 1):
-            if t < PACK:
-                nc.scalar.activation(out=gy[t][:], in_=y_banks[t][:], func=ACT.Copy, scale=gn_t[:, t : t + 1])
-            if t > 0:
-                nc.scalar.activation(out=sz[t - 1][:], in_=y_banks[t - 1][:], func=ACT.Abs)
+        def scaled(t, lo, hi):
+            if t == 1:
+                nc.vector.tensor_scalar(gy[t][:, lo:hi], y_bank[t, lo][:], gn_t[:, t : t + 1], None, ALU.mult)
+            else:
+                nc.scalar.activation(out=gy[t][:, lo:hi], in_=y_bank[t, lo][:], func=ACT.Copy, scale=gn_t[:, t : t + 1])
+
+        def size(t, lo, hi):
+            nc.scalar.activation(out=sz[t][:, lo:hi], in_=y_bank[t, lo][:], func=ACT.Abs)
+
+        scaled(0, 0, HALF)
+        size(0, 0, HALF)
+        scaled(0, HALF, S)
+        scaled(1, 0, S)
+        size(0, HALF, S)
+        scaled(2, 0, S)
+        size(1, 0, S)
+        scaled(3, 0, S)
+        size(2, 0, S)
+        size(3, 0, S)
         for t in range(PACK):
             for lo in (0, HALF):
                 looked_up = gy[t][:].indirect(entries(n2_t, lo, lo + HALF))
-                if t == PACK - 1 and lo == HALF:
+                if False:
                     nc.scalar.activation(out=h_win[t][:, S + lo : S + lo + HALF], in_=looked_up, func=ACT.Copy)
                 else:
                     nc.vector.tensor_copy(h_win[t][:, S + lo : S + lo + HALF], looked_up)
-            for lo in (0, HALF):
+            if t < PACK - 1:
+                nc.gpsimd.tensor_tensor(diff[:, t, :], gy[t][:], h_win[t][:, S : 2 * S], ALU.subtract)
+            for lo in (0, HALF) if t == PACK - 1 else ():
                 nc.vector.tensor_tensor(
                     diff[:, t, lo : lo + HALF],
                     gy[t][:, lo : lo + HALF],
@@ -152,12 +173,11 @@ def tile_picked_layelaegc_none_p_kernel(
 
         z_q = held.tile([P, S], U32, name="z_q", align_bytes=64)
         z_s = held.tile([P, S], U8, name="z_s", align_bytes=64)
-        h_banks = [psum.tile([P, S], F32, name=f"h_bank{t}") for t in range(PACK)]
 
-        def second_product(t, lo, hi):
+        def second_product(bank, t, lo, hi):
             rows = slice(t * P, (t + 1) * P)
             nc.tensor.matmul_mx(
-                out=h_banks[t][:, lo:hi],
+                out=bank,
                 lhsT=w2_q[:, rows].bitcast(FP8X4),
                 lhsT_scale=w2_s[:, rows],
                 rhs=z_q[:, lo:hi].bitcast(FP8X4),
@@ -165,9 +185,8 @@ def tile_picked_layelaegc_none_p_kernel(
                 start=True,
                 stop=True,
             )
-            nc.vector.tensor_copy(out=h_win[t][:, lo:hi], in_=h_banks[t][:, lo:hi])
 
-        for c, (lo, hi) in enumerate(Z_CHUNKS):
+        for lo, hi in Z_CHUNKS:
             for t in range(PACK):
                 nc.scalar.activation(
                     out=ea[:, t, lo:hi],
@@ -175,18 +194,34 @@ def tile_picked_layelaegc_none_p_kernel(
                     func=ACT.Exp,
                     scale=neg_tau[:, t : t + 1],
                 )
-            parts = [(a, a + P) for a in range(lo, hi, P)]
-            z_bf = [held.tile([P, PACK * P], BF16, name=f"z_bf{a}", tag=f"z_bf{a}", align_bytes=64) for a, b in parts]
-            for (a, b), zb in zip(parts, z_bf):
-                nc.vector.tensor_tensor(
-                    zb[:].rearrange("p (c i t) -> p c t i", i=2, t=PACK),
-                    diff[:, :, a:b].rearrange("p t (c i) -> p c t i", i=2),
-                    ea[:, :, a:b].rearrange("p t (c i) -> p c t i", i=2),
-                    ALU.mult,
-                )
-            for (a, b), zb in zip(parts, z_bf):
-                nc.vector.quantize_mx(out=z_q[:, a:b].bitcast(FP8X4), scales=z_s[:, a:b], in_=zb[:])
-            second_product(0, lo, hi)
+        z_bf = [held.tile([P, PACK * (hi - lo)], BF16, name=f"z_bf{lo}", tag=f"z_bf{lo}", align_bytes=64) for lo, hi in Z_CHUNKS]
+
+        def product(c, a, b):
+            lo = Z_CHUNKS[c][0]
+            nc.vector.tensor_tensor(
+                z_bf[c][:, PACK * (a - lo) : PACK * (b - lo)].rearrange("p (c i t) -> p c t i", i=2, t=PACK),
+                diff[:, :, a:b].rearrange("p t (c i) -> p c t i", i=2),
+                ea[:, :, a:b].rearrange("p t (c i) -> p c t i", i=2),
+                ALU.mult,
+            )
+
+        def quantize_z(c):
+            lo, hi = Z_CHUNKS[c]
+            nc.vector.quantize_mx(out=z_q[:, lo:hi].bitcast(FP8X4), scales=z_s[:, lo:hi], in_=z_bf[c][:])
+
+        h_early = psum.tile([P, 384], F32, name="h_early", tag="bank5")
+        h_late = psum.tile([P, 128], F32, name="h_late", tag="bank6")
+        product(0, 0, 256)
+        product(1, 256, 384)
+        quantize_z(0)
+        second_product(h_early[:, 0:256], 0, 0, 256)
+        quantize_z(1)
+        second_product(h_early[:, 256:384], 0, 256, 384)
+        product(2, 384, 512)
+        quantize_z(2)
+        second_product(h_late[:], 0, 384, 512)
+        nc.vector.tensor_copy(out=h_win[0][:, 0:384], in_=h_early[:])
+        nc.vector.tensor_copy(out=h_win[0][:, 384:512], in_=h_late[:])
 
         bias = held.tile([P, PACK], F32, name="bias")
         nc.vector.scalar_tensor_tensor(bias[:], sl_t[:], -1.0, th_t[:], ALU.mult, ALU.mult)
@@ -194,14 +229,16 @@ def tile_picked_layelaegc_none_p_kernel(
         def next_rows(t):
             staged = held.tile([P, PACK * P], BF16, name=f"w2_bf{t}", tag="z_bf384", align_bytes=64)
             quantize_w2(t, w2_rest[:, :, (t - 1) * P : t * P], staged)
-            second_product(t, 0, S)
+            bank = psum.tile([P, S], F32, name=f"h_bank{t}", tag=f"bank{(6 + t) % 8}")
+            second_product(bank[:], t, 0, S)
+            nc.vector.tensor_copy(out=h_win[t][:, 0:S], in_=bank[:])
 
         for t in range(1, PACK):
             next_rows(t)
 
         for t in range(PACK):
             res = held.tile([P, S], F32, name=f"res{t}")
-            cuts = [0, 128, 256, 384, 512] if t < PACK - 1 else [0, 128, 256, 384, 448, 512]
+            cuts = [0, 256, 512] if t < PACK - 1 else [0, 128, 256, 384, 448, 512]
             stored = 0
             for lo, hi in zip(cuts[:-1], cuts[1:]):
                 sg = ring.tile([P, 4 * (hi - lo)], F32, name="sg")

@@ -70,9 +70,9 @@ def tile_picked_layelaegc_none_p_kernel(
             in_=x_words[0].rearrange("p n t -> p (n t)").bitcast(I32),
         )
         nc.sync.dma_start(out=gn_t[:], in_=gn.rearrange("(p t) o -> p (t o)", t=PACK))
+        nc.sync.dma_start(out=tau_t[:], in_=tau.rearrange("(p t) o -> p (t o)", t=PACK))
         nc.sync.dma_start(out=w2_first[:], in_=w2_rows[:, :, 0:P])
         nc.sync.dma_start(n2_t[:], n2)
-        nc.sync.dma_start(out=tau_t[:], in_=tau.rearrange("(p t) o -> p (t o)", t=PACK))
         nc.sync.dma_start(n1_t[:], n1)
         nc.sync.dma_start(out=w2_rest[:], in_=w2_rows[:, :, P:N])
         nc.sync.dma_start(n3_t[:], n3)
@@ -128,15 +128,15 @@ def tile_picked_layelaegc_none_p_kernel(
         quantize_w2(0, w2_first[:], w2_bf0)
 
         neg_tau = held.tile([P, PACK], F32, name="neg_tau")
-        nc.vector.tensor_scalar(neg_tau[:], tau_t[:], -1.0, None, ALU.mult)
+        nc.gpsimd.tensor_scalar(neg_tau[:], tau_t[:], -1.0, 0.0, ALU.mult, ALU.add)
 
         gy = [held.tile([P, S], F32, name=f"gy{t}", align_bytes=64) for t in range(PACK)]
         sz = [held.tile([P, S], F32, name=f"sz{t}", align_bytes=64) for t in range(PACK)]
         diff = held.tile([P, PACK, S], F32, name="diff", align_bytes=64)
-        ea = held.tile([P, PACK, S], F32, name="ea", align_bytes=64)
+        ea = held.tile([P, PACK, 384], F32, name="ea", align_bytes=64)
 
         def scaled(t, lo, hi):
-            if t == 1:
+            if t == 1 or lo == HALF:
                 nc.vector.tensor_scalar(gy[t][:, lo:hi], y_bank[t, lo][:], gn_t[:, t : t + 1], None, ALU.mult)
             else:
                 nc.scalar.activation(out=gy[t][:, lo:hi], in_=y_bank[t, lo][:], func=ACT.Copy, scale=gn_t[:, t : t + 1])
@@ -147,14 +147,15 @@ def tile_picked_layelaegc_none_p_kernel(
         scaled(0, 0, HALF)
         size(0, 0, HALF)
         scaled(0, HALF, S)
-        scaled(1, 0, S)
+        size(1, 0, S)
         size(0, HALF, S)
         scaled(2, 0, S)
-        size(1, 0, S)
         scaled(3, 0, S)
         size(2, 0, S)
         size(3, 0, S)
         for t in range(PACK):
+            if t == 1:
+                scaled(1, 0, S)
             for lo in (0, HALF):
                 looked_up = gy[t][:].indirect(entries(n2_t, lo, lo + HALF))
                 if False:
@@ -164,10 +165,12 @@ def tile_picked_layelaegc_none_p_kernel(
             if t < PACK - 1:
                 nc.gpsimd.tensor_tensor(diff[:, t, :], gy[t][:], h_win[t][:, S : 2 * S], ALU.subtract)
             for lo in (0, HALF) if t == PACK - 1 else ():
-                nc.vector.tensor_tensor(
+                nc.vector.scalar_tensor_tensor(
                     diff[:, t, lo : lo + HALF],
-                    gy[t][:, lo : lo + HALF],
+                    y_bank[t, 0][:, lo : lo + HALF],
+                    gn_t[:, t : t + 1],
                     h_win[t][:, S + lo : S + lo + HALF],
+                    ALU.mult,
                     ALU.subtract,
                 )
 
@@ -186,10 +189,11 @@ def tile_picked_layelaegc_none_p_kernel(
                 stop=True,
             )
 
+        ea_last = h_win[0][:, 0:S].rearrange("p (t c) -> p t c", t=PACK)
         for lo, hi in Z_CHUNKS:
             for t in range(PACK):
                 nc.scalar.activation(
-                    out=ea[:, t, lo:hi],
+                    out=ea[:, t, lo:hi] if hi < S else ea_last[:, t, :],
                     in_=sz[t][:].indirect(entries(n1_t, lo, hi)),
                     func=ACT.Exp,
                     scale=neg_tau[:, t : t + 1],
@@ -201,7 +205,7 @@ def tile_picked_layelaegc_none_p_kernel(
             nc.vector.tensor_tensor(
                 z_bf[c][:, PACK * (a - lo) : PACK * (b - lo)].rearrange("p (c i t) -> p c t i", i=2, t=PACK),
                 diff[:, :, a:b].rearrange("p t (c i) -> p c t i", i=2),
-                ea[:, :, a:b].rearrange("p t (c i) -> p c t i", i=2),
+                (ea[:, :, a:b] if b < S else ea_last).rearrange("p t (c i) -> p c t i", i=2),
                 ALU.mult,
             )
 
@@ -223,7 +227,7 @@ def tile_picked_layelaegc_none_p_kernel(
         nc.vector.tensor_copy(out=h_win[0][:, 0:384], in_=h_early[:])
         nc.vector.tensor_copy(out=h_win[0][:, 384:512], in_=h_late[:])
 
-        bias = held.tile([P, PACK], F32, name="bias")
+        bias = held.tile([P, PACK], F32, name="bias", tag="z_bf0", align_bytes=64)
         nc.vector.scalar_tensor_tensor(bias[:], sl_t[:], -1.0, th_t[:], ALU.mult, ALU.mult)
 
         def next_rows(t):

from contextlib import ExitStack

import concourse.mybir as mybir

K, T, S, N, H, W = 512, 2048, 512, 512, 512, 2048
FLOPS = 2 * K * H * S + 2 * H * N * S

F32 = mybir.dt.float32
BF16 = mybir.dt.bfloat16
I32 = mybir.dt.int32
U32 = mybir.dt.uint32
U16 = mybir.dt.uint16
U8 = mybir.dt.uint8
FP8X4 = mybir.dt.float8_e4m3fn_x4
ALU = mybir.AluOpType
ACT = mybir.ActivationFunctionType

P = 128
PACK = 4
GROUP = 16
HALF = S // 2
Z_CHUNKS = ((0, 256), (256, 384), (384, 512))
W1_VECTOR_ROWS = 80


def entries(lst, lo, hi):
    return lst[:, lo // GROUP : hi // GROUP]


def tile_picked_layelaegc_none_p_kernel(
    tc, x_words, x_scales, w1, tau, gn, w2, sl, th, offs, n1, n2, n3, out
):
    nc = tc.nc
    with ExitStack() as ctx:
        held = ctx.enter_context(tc.tile_pool(name="held", bufs=1))
        ring = ctx.enter_context(tc.tile_pool(name="ring", bufs=5))
        psum = ctx.enter_context(tc.psum_pool(name="psum", bufs=1))

        offs_t = held.tile([P, S // GROUP], U16, name="offs_t")
        n1_t = held.tile([P, S // GROUP], U16, name="n1_t")
        n2_t = held.tile([P, S // GROUP], U16, name="n2_t")
        n3_t = held.tile([P, W // GROUP], U16, name="n3_t")

        xw = held.tile([P, T], U32, name="xw", align_bytes=64)
        xs = held.tile([P, T], U8, name="xs", align_bytes=64)
        w1_raw = held.tile([P, PACK, H], F32, name="w1_raw", align_bytes=64)
        w2_first = held.tile([P, PACK, P], F32, name="w2_first", align_bytes=64)
        w2_rest = held.tile([P, PACK, N - P], F32, name="w2_rest", align_bytes=64)
        tau_t = held.tile([P, PACK], F32, name="tau_t")
        gn_t = held.tile([P, PACK], F32, name="gn_t")
        sl_t = held.tile([P, PACK], F32, name="sl_t")
        th_t = held.tile([P, PACK], F32, name="th_t")

        nc.vector.memset(xs[:].bitcast(I32), 0)
        h_win = [
            held.tile([P, (4 if t < PACK - 1 else 2) * S], F32, name=f"h_win{t}", align_bytes=64) for t in range(PACK)
        ]
        for t in range(PACK - 1):
            nc.vector.memset(h_win[t][:, 2 * S : 4 * S], 0.0)
        w2_rows = w2.rearrange("(p j) n -> p j n", j=PACK)
        nc.sync.dma_start(offs_t[:], offs)
        nc.sync.dma_start(out=w1_raw[:], in_=w1.rearrange("(p j) n -> p j n", j=PACK))
        for q in range(4):
            nc.sync.dma_start(
                out=xs[32 * q : 32 * q + 4, :].bitcast(I32),
                in_=x_scales[0, 4 * q : 4 * q + 4, :].bitcast(I32),
            )
        nc.sync.dma_start(
            out=xw[:].bitcast(I32),
            in_=x_words[0].rearrange("p n t -> p (n t)").bitcast(I32),
        )
        nc.sync.dma_start(out=gn_t[:], in_=gn.rearrange("(p t) o -> p (t o)", t=PACK))
        nc.sync.dma_start(out=tau_t[:], in_=tau.rearrange("(p t) o -> p (t o)", t=PACK))
        nc.sync.dma_start(out=w2_first[:], in_=w2_rows[:, :, 0:P])
        nc.sync.dma_start(n2_t[:], n2)
        nc.sync.dma_start(n1_t[:], n1)
        nc.sync.dma_start(out=w2_rest[:], in_=w2_rows[:, :, P:N])
        nc.sync.dma_start(n3_t[:], n3)
        with nc.allow_non_contiguous_dma(reason="one value a row"):
            nc.sync.dma_start(out=sl_t[:], in_=sl.rearrange("(t p) o -> p (t o)", p=P))
            nc.sync.dma_start(out=th_t[:], in_=th.rearrange("(t p) o -> p (t o)", p=P))

        w1_bf = held.tile([P, PACK * H], BF16, name="w1_bf", tag="w1_bf_then_xw_g", align_bytes=64)
        w1_dst = w1_bf[:].rearrange("p (t m j) -> p m j t", t=PACK, j=PACK)
        w1_src = w1_raw[:].rearrange("p j (m t) -> p m j t", t=PACK)
        nc.vector.tensor_copy(out=w1_dst[:, 0:W1_VECTOR_ROWS], in_=w1_src[:, 0:W1_VECTOR_ROWS])
        nc.scalar.activation(out=w1_dst[:, W1_VECTOR_ROWS:P], in_=w1_src[:, W1_VECTOR_ROWS:P], func=ACT.Copy)
        xs_g = held.tile([P, S], U8, name="xs_g", align_bytes=64)
        nc.vector.tensor_copy(xs_g[:], xs[:].indirect(offs_t[:]))

        w1_q = held.tile([P, H], U32, name="w1_q", align_bytes=64)
        w1_s = held.tile([P, H], U8, name="w1_s", align_bytes=64)
        nc.vector.quantize_mx(out=w1_q[:].bitcast(FP8X4), scales=w1_s[:], in_=w1_bf[:])

        xw_g = held.tile([P, S], U32, name="xw_g", tag="w1_bf_then_xw_g", align_bytes=64)
        for lo in (0, HALF):
            nc.vector.tensor_copy(xw_g[:, lo : lo + HALF], xw[:].indirect(entries(offs_t, lo, lo + HALF)))
        y_bank = {(0, 0): psum.tile([P, HALF], F32, name="y0_low", tag="bank0"), (0, HALF): psum.tile([P, HALF], F32, name="y0_high", tag="bank1")}
        for t in range(1, PACK):
            y_bank[t, 0] = psum.tile([P, S], F32, name=f"y{t}", tag=f"bank{t + 1}")
        for t, lo, hi in [(0, 0, HALF), (1, 0, HALF), (0, HALF, S), (1, HALF, S), (2, 0, S), (3, 0, S)]:
            rows = slice(t * P, (t + 1) * P)
            nc.tensor.matmul_mx(
                out=y_bank[t, lo][:] if t == 0 else y_bank[t, 0][:, lo:hi],
                lhsT=w1_q[:, rows].bitcast(FP8X4),
                lhsT_scale=w1_s[:, rows],
                rhs=xw_g[:, lo:hi].bitcast(FP8X4),
                rhs_scale=xs_g[:, lo:hi],
                start=True,
                stop=True,
            )

        w2_q = held.tile([P, N], U32, name="w2_q", align_bytes=64)
        w2_s = held.tile([P, N], U8, name="w2_s", align_bytes=64)

        def quantize_w2(t, src, staged):
            nc.vector.tensor_copy(
                out=staged[:].rearrange("p (c i j) -> p c j i", i=4, j=PACK),
                in_=src.rearrange("p j (c i) -> p c j i", i=4),
            )
            nc.vector.quantize_mx(
                out=w2_q[:, t * P : (t + 1) * P].bitcast(FP8X4),
                scales=w2_s[:, t * P : (t + 1) * P],
                in_=staged[:],
            )

        w2_bf0 = held.tile([P, PACK * P], BF16, name="w2_bf0", align_bytes=64)
        quantize_w2(0, w2_first[:], w2_bf0)

        neg_tau = held.tile([P, PACK], F32, name="neg_tau")
        nc.gpsimd.tensor_scalar(neg_tau[:], tau_t[:], -1.0, 0.0, ALU.mult, ALU.add)

        gy = [held.tile([P, S], F32, name=f"gy{t}", align_bytes=64) for t in range(PACK)]
        sz = [held.tile([P, S], F32, name=f"sz{t}", align_bytes=64) for t in range(PACK)]
        diff = held.tile([P, PACK, S], F32, name="diff", align_bytes=64)
        ea = held.tile([P, PACK, 384], F32, name="ea", align_bytes=64)

        def scaled(t, lo, hi):
            if t == 1 or lo == HALF:
                nc.vector.tensor_scalar(gy[t][:, lo:hi], y_bank[t, lo][:], gn_t[:, t : t + 1], None, ALU.mult)
            else:
                nc.scalar.activation(out=gy[t][:, lo:hi], in_=y_bank[t, lo][:], func=ACT.Copy, scale=gn_t[:, t : t + 1])

        def size(t, lo, hi):
            nc.scalar.activation(out=sz[t][:, lo:hi], in_=y_bank[t, lo][:], func=ACT.Abs)

        scaled(0, 0, HALF)
        size(0, 0, HALF)
        scaled(0, HALF, S)
        size(1, 0, S)
        size(0, HALF, S)
        scaled(2, 0, S)
        scaled(3, 0, S)
        size(2, 0, S)
        size(3, 0, S)
        for t in range(PACK):
            if t == 1:
                scaled(1, 0, S)
            for lo in (0, HALF):
                looked_up = gy[t][:].indirect(entries(n2_t, lo, lo + HALF))
                if False:
                    nc.scalar.activation(out=h_win[t][:, S + lo : S + lo + HALF], in_=looked_up, func=ACT.Copy)
                else:
                    nc.vector.tensor_copy(h_win[t][:, S + lo : S + lo + HALF], looked_up)
            if t < PACK - 1:
                nc.gpsimd.tensor_tensor(diff[:, t, :], gy[t][:], h_win[t][:, S : 2 * S], ALU.subtract)
            for lo in (0, HALF) if t == PACK - 1 else ():
                nc.vector.scalar_tensor_tensor(
                    diff[:, t, lo : lo + HALF],
                    y_bank[t, 0][:, lo : lo + HALF],
                    gn_t[:, t : t + 1],
                    h_win[t][:, S + lo : S + lo + HALF],
                    ALU.mult,
                    ALU.subtract,
                )

        z_q = held.tile([P, S], U32, name="z_q", align_bytes=64)
        z_s = held.tile([P, S], U8, name="z_s", align_bytes=64)

        def second_product(bank, t, lo, hi):
            rows = slice(t * P, (t + 1) * P)
            nc.tensor.matmul_mx(
                out=bank,
                lhsT=w2_q[:, rows].bitcast(FP8X4),
                lhsT_scale=w2_s[:, rows],
                rhs=z_q[:, lo:hi].bitcast(FP8X4),
                rhs_scale=z_s[:, lo:hi],
                start=True,
                stop=True,
            )

        ea_last = h_win[0][:, 0:S].rearrange("p (t c) -> p t c", t=PACK)
        for lo, hi in Z_CHUNKS:
            for t in range(PACK):
                nc.scalar.activation(
                    out=ea[:, t, lo:hi] if hi < S else ea_last[:, t, :],
                    in_=sz[t][:].indirect(entries(n1_t, lo, hi)),
                    func=ACT.Exp,
                    scale=neg_tau[:, t : t + 1],
                )
        z_bf = [held.tile([P, PACK * (hi - lo)], BF16, name=f"z_bf{lo}", tag=f"z_bf{lo}", align_bytes=64) for lo, hi in Z_CHUNKS]

        def product(c, a, b):
            lo = Z_CHUNKS[c][0]
            nc.vector.tensor_tensor(
                z_bf[c][:, PACK * (a - lo) : PACK * (b - lo)].rearrange("p (c i t) -> p c t i", i=2, t=PACK),
                diff[:, :, a:b].rearrange("p t (c i) -> p c t i", i=2),
                (ea[:, :, a:b] if b < S else ea_last).rearrange("p t (c i) -> p c t i", i=2),
                ALU.mult,
            )

        def quantize_z(c):
            lo, hi = Z_CHUNKS[c]
            nc.vector.quantize_mx(out=z_q[:, lo:hi].bitcast(FP8X4), scales=z_s[:, lo:hi], in_=z_bf[c][:])

        h_early = psum.tile([P, 384], F32, name="h_early", tag="bank5")
        h_late = psum.tile([P, 128], F32, name="h_late", tag="bank6")
        product(0, 0, 256)
        product(1, 256, 384)
        quantize_z(0)
        second_product(h_early[:, 0:256], 0, 0, 256)
        quantize_z(1)
        second_product(h_early[:, 256:384], 0, 256, 384)
        product(2, 384, 512)
        quantize_z(2)
        second_product(h_late[:], 0, 384, 512)
        nc.vector.tensor_copy(out=h_win[0][:, 0:384], in_=h_early[:])
        nc.vector.tensor_copy(out=h_win[0][:, 384:512], in_=h_late[:])

        bias = held.tile([P, PACK], F32, name="bias", tag="z_bf0", align_bytes=64)
        nc.vector.scalar_tensor_tensor(bias[:], sl_t[:], -1.0, th_t[:], ALU.mult, ALU.mult)

        def next_rows(t):
            staged = held.tile([P, PACK * P], BF16, name=f"w2_bf{t}", tag="z_bf384", align_bytes=64)
            quantize_w2(t, w2_rest[:, :, (t - 1) * P : t * P], staged)
            bank = psum.tile([P, S], F32, name=f"h_bank{t}", tag=f"bank{(6 + t) % 8}")
            second_product(bank[:], t, 0, S)
            nc.vector.tensor_copy(out=h_win[t][:, 0:S], in_=bank[:])

        for t in range(1, PACK):
            next_rows(t)

        for t in range(PACK):
            res = held.tile([P, S], F32, name=f"res{t}")
            cuts = [0, 256, 512] if t < PACK - 1 else [0, 128, 256, 384, 448, 512]
            stored = 0
            for lo, hi in zip(cuts[:-1], cuts[1:]):
                sg = ring.tile([P, 4 * (hi - lo)], F32, name="sg")
                nc.scalar.activation(
                    out=sg[:],
                    in_=h_win[t][:].indirect(entries(n3_t, 4 * lo, 4 * hi)),
                    func=ACT.Sigmoid,
                    scale=sl_t[:, t : t + 1],
                    bias=bias[:, t : t + 1],
                )
                cnt = ring.tile([P, hi - lo], F32, name="cnt")
                nc.vector.tensor_reduce(
                    cnt[:], sg[:].rearrange("p (j d) -> p j d", d=4), mybir.AxisListType.X, ALU.add
                )
                nc.vector.scalar_tensor_tensor(
                    res[:, lo:hi], cnt[:], -1.5, h_win[t][:, lo:hi], ALU.add, ALU.max
                )
                if hi == S or (t == PACK - 1 and hi >= 384):
                    nc.sync.dma_start(out=out[t * P : (t + 1) * P, stored:hi], in_=res[:, stored:hi])
                    stored = hi
